import numpy as np
import ml_dtypes


def mxq(x, axis, fmt="e4m3"):
    dtype, down = {"e4m3": (ml_dtypes.float8_e4m3fn, 7), "e5m2": (ml_dtypes.float8_e5m2, 14)}[fmt]
    v = np.moveaxis(np.asarray(x, np.float32).astype(ml_dtypes.bfloat16).astype(np.float64), axis, -1)
    blocks = v.reshape(v.shape[:-1] + (-1, 32))
    amax = np.abs(blocks).max(-1, keepdims=True)
    byte = np.maximum(np.where(amax > 0, np.frexp(amax)[1] - 1 + 127, 0) - down, 1)
    scale = np.exp2(byte - 127.0)
    codes = (blocks / scale).astype(np.float32).astype(dtype).astype(np.float64)
    return np.moveaxis((codes * scale).reshape(v.shape), -1, axis)


WIDE = False


def mx_kscale(k, group=512):
    if not WIDE:
        return np.ones(k)
    levels = np.array([10, -10, 5, -5, 0])
    if group != 512:
        return np.exp2(np.random.permutation(np.resize(levels, k // group))).repeat(group)
    if k % 512:
        return np.exp2(np.random.permutation(np.resize(levels, k // 32))).repeat(32)
    a = np.empty((k // 512, 16))
    for p in range(k // 512):
        a[p, :8] = np.random.permutation(np.resize(levels, 8))
        for g in range(8):
            far = levels[np.abs(levels - a[p, g]) >= 10]
            a[p, g + 8] = far[np.random.randint(len(far))]
    return np.exp2(a.ravel()).repeat(32)


def f64(x):
    return np.asarray(x).astype(np.float64)


G, D, M, N = 2, 256, 128, 512


def setup_inputs():
    n = np.random.standard_normal
    s_d = mx_kscale(D, 0)
    return {
        "x": (n((G, D, N)) * s_d[:, None]).astype(np.float32),
        "w1": (n((G, D, M)) / np.sqrt(D) / s_d[:, None]).astype(np.float32),
        "w2": (n((G, D, M)) / np.sqrt(D) / s_d[:, None]).astype(np.float32),
        "w3": (n((G, D, M)) / np.sqrt(D) / s_d[:, None]).astype(np.float32),
        "dx": (n((G, D, N)) * s_d[:, None]).astype(np.float32),
        "og": (np.random.uniform(0.5, 2.0, (G, M, 1))).astype(np.float32),
        "base": (0.3 * n((G, M, N))).astype(np.float32),
    }


def reference(x, w1, w2, w3, dx, og, base):
    w1q = mxq(f64(w1), 1, "e4m3")
    xq = mxq(f64(x), 1, "e4m3")
    z1 = w1q.transpose(0, 2, 1) @ xq
    dxq = mxq(f64(dx), 1, "e4m3")
    tz1 = w1q.transpose(0, 2, 1) @ dxq
    w2q = mxq(f64(w2), 1, "e4m3")
    z2 = w2q.transpose(0, 2, 1) @ xq
    tz2 = w2q.transpose(0, 2, 1) @ dxq
    w3q = mxq(f64(w3), 1, "e4m3")
    z3 = w3q.transpose(0, 2, 1) @ xq
    tz3 = w3q.transpose(0, 2, 1) @ dxq
    se = np.exp(z1) + np.exp(z2) + np.exp(z3)
    xse = tz1 * np.exp(z1) + tz2 * np.exp(z2) + tz3 * np.exp(z3)
    xh = xse / se * np.tanh(z1) + tz1 * (1.0 - np.square(np.tanh(z1))) * np.log(se)
    y = xh * f64(og) + f64(base)
    return y

@@ -1,0 +1,172 @@
+from contextlib import ExitStack
+
+import concourse.mybir as mybir
+
+G, D, M, N = 2, 256, 128, 512
+FLOPS = 6 * 2 * G * D * M * N
+
+F32 = mybir.dt.float32
+BF16 = mybir.dt.bfloat16
+U32 = mybir.dt.uint32
+U8 = mybir.dt.uint8
+FP8X4 = mybir.dt.float8_e4m3fn_x4
+ACT = mybir.ActivationFunctionType
+ALU = mybir.AluOpType
+
+P = 128
+PACK = 4
+ROWS = D // PACK
+RUN = 4
+HALF = N // 2
+X_VECTOR_COLS = 336
+
+
+def by_partition(src):
+    return src.rearrange("g (p j) c -> (g p) j c", j=PACK)
+
+
+def interleave(copy, packed, raw, cols):
+    copy(
+        out=packed[:, cols, :].rearrange("p (c i) j -> p c j i", i=RUN),
+        in_=raw[:, :, cols].rearrange("p j (c i) -> p c j i", i=RUN),
+    )
+
+
+def quantize(nc, codes, scales, packed):
+    nc.vector.quantize_mx(
+        out=codes.bitcast(FP8X4), scales=scales, in_=packed[:].rearrange("p c j -> p (c j)")
+    )
+
+
+def tile_rows_tnsoftmaxthree_kernel(tc, x, w1, w2, w3, dx, og, base, out):
+    nc = tc.nc
+    groups = range(G)
+
+    with ExitStack() as ctx:
+        sb = ctx.enter_context(tc.tile_pool(name="sb", bufs=1))
+        ps = ctx.enter_context(tc.psum_pool(name="ps", bufs=1))
+        ctx.enter_context(tc.manual_schedule())
+
+        def per_group(name):
+            return [sb.tile([P, N], F32, name="%s%d" % (name, g)) for g in groups]
+
+        x_raw = sb.tile([P, PACK, N], F32)
+        nc.sync.dma_start(out=x_raw[:], in_=by_partition(x))
+        w_raw = []
+        for b, w in enumerate((w1, w2, w3)):
+            w_raw.append(sb.tile([P, PACK, M], F32, name="w_raw%d" % b))
+            nc.sync.dma_start(out=w_raw[b][:], in_=by_partition(w))
+        dx_raw = []
+        for h in range(2):
+            dx_raw.append(sb.tile([P, PACK, HALF], F32, name="dx_raw%d" % h))
+            nc.sync.dma_start(out=dx_raw[h][:], in_=by_partition(dx)[:, :, h * HALF : (h + 1) * HALF])
+        base_sb = sb.tile([P, G, N], F32)
+        nc.sync.dma_start(out=base_sb[:], in_=base.rearrange("g m n -> m g n"))
+        gain = sb.tile([P, G], F32)
+        with nc.allow_non_contiguous_dma(reason="one gain per output feature, one per partition"):
+            nc.sync.dma_start(out=gain[:], in_=og.rearrange("g m o -> m (g o)"))
+
+        x_bf = sb.tile([P, N, PACK], BF16, align_bytes=64)
+        x_codes = sb.tile([P, N], U32, align_bytes=64)
+        x_scales = sb.tile([P, N], U8, align_bytes=64)
+        dx_bf = [sb.tile([P, HALF, PACK], BF16, align_bytes=64, name="dx_bf%d" % h) for h in range(2)]
+        dx_codes = sb.tile([P, N], U32, align_bytes=64)
+        dx_scales = sb.tile([P, N], U8, align_bytes=64)
+        w_bf = [sb.tile([P, M, PACK], BF16, align_bytes=64, name="w_bf%d" % b) for b in range(3)]
+        w_codes = [sb.tile([P, M], U32, align_bytes=64, name="w_codes%d" % b) for b in range(3)]
+        w_scales = [sb.tile([P, M], U8, align_bytes=64, name="w_scales%d" % b) for b in range(3)]
+
+        bank = [[ps.tile([P, N], F32, name="bank%d_%d" % (g, i)) for i in range(4)] for g in groups]
+        z = [[bank[g][0], bank[g][1], bank[g][2]] for g in groups]
+        tz = [[bank[g][3], bank[g][1], bank[g][2]] for g in groups]
+
+        def product(acc, g, b, codes, scales):
+            rows = slice(g * ROWS, (g + 1) * ROWS)
+            nc.tensor.matmul_mx(
+                out=acc[:],
+                lhsT=w_codes[b][rows, :].bitcast(FP8X4),
+                lhsT_scale=w_scales[b][rows, :],
+                rhs=codes[rows, :].bitcast(FP8X4),
+                rhs_scale=scales[rows, :],
+                start=True,
+                stop=True,
+            )
+
+        every = slice(None)
+        interleave(nc.vector.tensor_copy, x_bf, x_raw, slice(0, X_VECTOR_COLS))
+        interleave(nc.scalar.copy, x_bf, x_raw, slice(X_VECTOR_COLS, N))
+        interleave(nc.scalar.copy, w_bf[0], w_raw[0], every)
+        interleave(nc.scalar.copy, w_bf[1], w_raw[1], every)
+        quantize(nc, x_codes[:], x_scales[:], x_bf)
+        quantize(nc, w_codes[0][:], w_scales[0][:], w_bf[0])
+        interleave(nc.vector.tensor_copy, w_bf[2], w_raw[2], every)
+        quantize(nc, w_codes[1][:], w_scales[1][:], w_bf[1])
+        quantize(nc, w_codes[2][:], w_scales[2][:], w_bf[2])
+
+        e = [per_group("e1_"), per_group("e2_"), per_group("e3_")]
+        for b in range(3):
+            for g in groups:
+                product(z[g][b], g, b, x_codes, x_scales)
+                nc.scalar.activation(out=e[b][g][:], in_=z[g][b][:], func=ACT.Exp)
+        th, th2 = per_group("th"), per_group("th2")
+        for g in groups:
+            nc.scalar.activation(out=th[g][:], in_=z[g][0][:], func=ACT.Tanh)
+        for g in groups:
+            nc.scalar.activation(out=th2[g][:], in_=th[g][:], func=ACT.Square)
+
+        for h in range(2):
+            cols = slice(h * HALF, (h + 1) * HALF)
+            interleave(nc.vector.tensor_copy, dx_bf[h], dx_raw[h], every)
+            quantize(nc, dx_codes[:, cols], dx_scales[:, cols], dx_bf[h])
+        for g in groups:
+            for b in range(2):
+                product(tz[g][b], g, b, dx_codes, dx_scales)
+        for g in groups:
+            product(tz[g][2], g, 2, dx_codes, dx_scales)
+
+        e12, se = per_group("e12_"), per_group("se")
+        for g in groups:
+            nc.vector.tensor_tensor(out=e12[g][:], in0=e[0][g][:], in1=e[1][g][:], op=ALU.add)
+        for g in groups:
+            nc.vector.tensor_tensor(out=se[g][:], in0=e12[g][:], in1=e[2][g][:], op=ALU.add)
+
+        lse, inv = per_group("lse"), per_group("inv")
+        for g in groups:
+            nc.scalar.activation(out=lse[g][:], in_=se[g][:], func=ACT.Ln)
+        for g in groups:
+            nc.scalar.activation(out=inv[g][:], in_=lse[g][:], func=ACT.Exp, scale=-1.0)
+
+        a = [per_group("a1_"), per_group("a2_"), per_group("a3_")]
+        for g in groups:
+            for b in range(2):
+                nc.vector.tensor_tensor(out=a[b][g][:], in0=tz[g][b][:], in1=e[b][g][:], op=ALU.mult)
+        for g in groups:
+            nc.vector.tensor_tensor(out=a[2][g][:], in0=tz[g][2][:], in1=e[2][g][:], op=ALU.mult)
+        dth = per_group("dth")
+        for g in groups:
+            nc.vector.scalar_tensor_tensor(
+                out=dth[g][:], in0=th2[g][:], scalar=-1.0, in1=tz[g][0][:], op0=ALU.add, op1=ALU.mult
+            )
+        a12, xse = per_group("a12_"), per_group("xse")
+        for g in groups:
+            nc.vector.tensor_tensor(out=a12[g][:], in0=a[0][g][:], in1=a[1][g][:], op=ALU.add)
+        for g in groups:
+            nc.vector.tensor_tensor(out=xse[g][:], in0=a12[g][:], in1=a[2][g][:], op=ALU.add)
+        second, rest, first, ratio, y = (per_group(s) for s in ("second", "rest", "first", "ratio", "y"))
+        for g in groups:
+            nc.vector.scalar_tensor_tensor(
+                out=second[g][:], in0=dth[g][:], scalar=gain[:, g : g + 1], in1=lse[g][:],
+                op0=ALU.mult, op1=ALU.mult,
+            )
+        for g in groups:
+            nc.vector.scalar_tensor_tensor(
+                out=first[g][:], in0=xse[g][:], scalar=gain[:, g : g + 1], in1=th[g][:],
+                op0=ALU.mult, op1=ALU.mult,
+            )
+        for g in groups:
+            nc.vector.tensor_tensor(out=rest[g][:], in0=base_sb[:, g, :], in1=second[g][:], op=ALU.subtract)
+        for g in groups:
+            nc.vector.tensor_tensor(out=ratio[g][:], in0=first[g][:], in1=inv[g][:], op=ALU.mult)
+        for g in groups:
+            nc.vector.tensor_tensor(out=y[g][:], in0=ratio[g][:], in1=rest[g][:], op=ALU.add)
+            nc.sync.dma_start(out=out[g], in_=y[g][:])

@@ -18,17 +18,17 @@ PACK = 4
 ROWS = D // PACK
 RUN = 4
 HALF = N // 2
-X_VECTOR_COLS = 336
+X_VECTOR_COLS = 168
 
 
 def by_partition(src):
     return src.rearrange("g (p j) c -> (g p) j c", j=PACK)
 
 
-def interleave(copy, packed, raw, cols):
+def interleave(copy, packed, raw):
     copy(
-        out=packed[:, cols, :].rearrange("p (c i) j -> p c j i", i=RUN),
-        in_=raw[:, :, cols].rearrange("p j (c i) -> p c j i", i=RUN),
+        out=packed.rearrange("p (c i) j -> p c j i", i=RUN),
+        in_=raw.rearrange("p j (c i) -> p c j i", i=RUN),
     )
 
 
@@ -50,23 +50,24 @@ def tile_rows_tnsoftmaxthree_kernel(tc, x, w1, w2, w3, dx, og, base, out):
         def per_group(name):
             return [sb.tile([P, N], F32, name="%s%d" % (name, g)) for g in groups]
 
-        x_raw = sb.tile([P, PACK, N], F32)
-        nc.sync.dma_start(out=x_raw[:], in_=by_partition(x))
-        w_raw = []
-        for b, w in enumerate((w1, w2, w3)):
-            w_raw.append(sb.tile([P, PACK, M], F32, name="w_raw%d" % b))
-            nc.sync.dma_start(out=w_raw[b][:], in_=by_partition(w))
-        dx_raw = []
+        halves = [slice(h * HALF, (h + 1) * HALF) for h in range(2)]
+        w_raw = [sb.tile([P, PACK, M], F32, name="w_raw%d" % b) for b in range(3)]
+        x_raw = [sb.tile([P, PACK, HALF], F32, name="x_raw%d" % h) for h in range(2)]
+        dx_raw = [sb.tile([P, PACK, HALF], F32, name="dx_raw%d" % h) for h in range(2)]
+        nc.sync.dma_start(out=w_raw[0][:], in_=by_partition(w1))
         for h in range(2):
-            dx_raw.append(sb.tile([P, PACK, HALF], F32, name="dx_raw%d" % h))
-            nc.sync.dma_start(out=dx_raw[h][:], in_=by_partition(dx)[:, :, h * HALF : (h + 1) * HALF])
+            nc.sync.dma_start(out=x_raw[h][:], in_=by_partition(x)[:, :, halves[h]])
+        nc.sync.dma_start(out=w_raw[1][:], in_=by_partition(w2))
+        nc.sync.dma_start(out=w_raw[2][:], in_=by_partition(w3))
+        for h in range(2):
+            nc.sync.dma_start(out=dx_raw[h][:], in_=by_partition(dx)[:, :, halves[h]])
         base_sb = sb.tile([P, G, N], F32)
         nc.sync.dma_start(out=base_sb[:], in_=base.rearrange("g m n -> m g n"))
         gain = sb.tile([P, G], F32)
         with nc.allow_non_contiguous_dma(reason="one gain per output feature, one per partition"):
             nc.sync.dma_start(out=gain[:], in_=og.rearrange("g m o -> m (g o)"))
 
-        x_bf = sb.tile([P, N, PACK], BF16, align_bytes=64)
+        x_bf = [sb.tile([P, HALF, PACK], BF16, align_bytes=64, name="x_bf%d" % h) for h in range(2)]
         x_codes = sb.tile([P, N], U32, align_bytes=64)
         x_scales = sb.tile([P, N], U8, align_bytes=64)
         dx_bf = [sb.tile([P, HALF, PACK], BF16, align_bytes=64, name="dx_bf%d" % h) for h in range(2)]
@@ -92,14 +93,16 @@ def tile_rows_tnsoftmaxthree_kernel(tc, x, w1, w2, w3, dx, og, base, out):
                 stop=True,
             )
 
-        every = slice(None)
-        interleave(nc.vector.tensor_copy, x_bf, x_raw, slice(0, X_VECTOR_COLS))
-        interleave(nc.scalar.copy, x_bf, x_raw, slice(X_VECTOR_COLS, N))
-        interleave(nc.scalar.copy, w_bf[0], w_raw[0], every)
-        interleave(nc.scalar.copy, w_bf[1], w_raw[1], every)
-        quantize(nc, x_codes[:], x_scales[:], x_bf)
+        interleave(nc.scalar.copy, w_bf[0][:], w_raw[0][:])
         quantize(nc, w_codes[0][:], w_scales[0][:], w_bf[0])
-        interleave(nc.vector.tensor_copy, w_bf[2], w_raw[2], every)
+        interleave(nc.vector.tensor_copy, x_bf[0][:, :X_VECTOR_COLS, :], x_raw[0][:, :, :X_VECTOR_COLS])
+        interleave(nc.scalar.copy, x_bf[0][:, X_VECTOR_COLS:, :], x_raw[0][:, :, X_VECTOR_COLS:])
+        quantize(nc, x_codes[:, halves[0]], x_scales[:, halves[0]], x_bf[0])
+        interleave(nc.vector.tensor_copy, x_bf[1][:, :X_VECTOR_COLS, :], x_raw[1][:, :, :X_VECTOR_COLS])
+        interleave(nc.scalar.copy, x_bf[1][:, X_VECTOR_COLS:, :], x_raw[1][:, :, X_VECTOR_COLS:])
+        quantize(nc, x_codes[:, halves[1]], x_scales[:, halves[1]], x_bf[1])
+        interleave(nc.scalar.copy, w_bf[1][:], w_raw[1][:])
+        interleave(nc.vector.tensor_copy, w_bf[2][:], w_raw[2][:])
         quantize(nc, w_codes[1][:], w_scales[1][:], w_bf[1])
         quantize(nc, w_codes[2][:], w_scales[2][:], w_bf[2])
 
@@ -115,9 +118,8 @@ def tile_rows_tnsoftmaxthree_kernel(tc, x, w1, w2, w3, dx, og, base, out):
             nc.scalar.activation(out=th2[g][:], in_=th[g][:], func=ACT.Square)
 
         for h in range(2):
-            cols = slice(h * HALF, (h + 1) * HALF)
-            interleave(nc.vector.tensor_copy, dx_bf[h], dx_raw[h], every)
-            quantize(nc, dx_codes[:, cols], dx_scales[:, cols], dx_bf[h])
+            interleave(nc.vector.tensor_copy, dx_bf[h][:], dx_raw[h][:])
+            quantize(nc, dx_codes[:, halves[h]], dx_scales[:, halves[h]], dx_bf[h])
         for g in groups:
             for b in range(2):
                 product(tz[g][b], g, b, dx_codes, dx_scales)
@@ -128,7 +130,7 @@ def tile_rows_tnsoftmaxthree_kernel(tc, x, w1, w2, w3, dx, og, base, out):
         for g in groups:
             nc.vector.tensor_tensor(out=e12[g][:], in0=e[0][g][:], in1=e[1][g][:], op=ALU.add)
         for g in groups:
-            nc.vector.tensor_tensor(out=se[g][:], in0=e12[g][:], in1=e[2][g][:], op=ALU.add)
+            nc.gpsimd.tensor_tensor(out=se[g][:], in0=e12[g][:], in1=e[2][g][:], op=ALU.add)
 
         lse, inv = per_group("lse"), per_group("inv")
         for g in groups:
@@ -149,7 +151,7 @@ def tile_rows_tnsoftmaxthree_kernel(tc, x, w1, w2, w3, dx, og, base, out):
             )
         a12, xse = per_group("a12_"), per_group("xse")
         for g in groups:
-            nc.vector.tensor_tensor(out=a12[g][:], in0=a[0][g][:], in1=a[1][g][:], op=ALU.add)
+            nc.gpsimd.tensor_tensor(out=a12[g][:], in0=a[0][g][:], in1=a[1][g][:], op=ALU.add)
         for g in groups:
             nc.vector.tensor_tensor(out=xse[g][:], in0=a12[g][:], in1=a[2][g][:], op=ALU.add)
         second, rest, first, ratio, y = (per_group(s) for s in ("second", "rest", "first", "ratio", "y"))
@@ -163,10 +165,23 @@ def tile_rows_tnsoftmaxthree_kernel(tc, x, w1, w2, w3, dx, og, base, out):
                 out=first[g][:], in0=xse[g][:], scalar=gain[:, g : g + 1], in1=th[g][:],
                 op0=ALU.mult, op1=ALU.mult,
             )
-        for g in groups:
+
+        def add_base(g):
             nc.vector.tensor_tensor(out=rest[g][:], in0=base_sb[:, g, :], in1=second[g][:], op=ALU.subtract)
-        for g in groups:
-            nc.vector.tensor_tensor(out=ratio[g][:], in0=first[g][:], in1=inv[g][:], op=ALU.mult)
-        for g in groups:
-            nc.vector.tensor_tensor(out=y[g][:], in0=ratio[g][:], in1=rest[g][:], op=ALU.add)
-            nc.sync.dma_start(out=out[g], in_=y[g][:])
+
+        def divide(g, cols):
+            nc.vector.tensor_tensor(out=ratio[g][:, cols], in0=first[g][:, cols], in1=inv[g][:, cols], op=ALU.mult)
+
+        def finish(g, cols, queue):
+            nc.vector.tensor_tensor(out=y[g][:, cols], in0=ratio[g][:, cols], in1=rest[g][:, cols], op=ALU.add)
+            queue.dma_start(out=out[g, :, cols], in_=y[g][:, cols])
+
+        whole, head, tail = slice(0, N), slice(0, N - M), slice(N - M, N)
+        add_base(0)
+        divide(0, whole)
+        add_base(1)
+        finish(0, whole, nc.sync)
+        divide(1, head)
+        divide(1, tail)
+        finish(1, head, nc.scalar)
+        finish(1, tail, nc.sync)

@@ -18,7 +18,7 @@ PACK = 4
 ROWS = D // PACK
 RUN = 4
 HALF = N // 2
-X_VECTOR_COLS = 168
+POOL_COLS = 768
 
 
 def by_partition(src):
@@ -30,6 +30,10 @@ def interleave(copy, packed, raw):
         out=packed.rearrange("p (c i) j -> p c j i", i=RUN),
         in_=raw.rearrange("p j (c i) -> p c j i", i=RUN),
     )
+
+
+def flat(tile):
+    return tile[:].rearrange("p g n -> p (g n)")
 
 
 def quantize(nc, codes, scales, packed):
@@ -50,27 +54,32 @@ def tile_rows_tnsoftmaxthree_kernel(tc, x, w1, w2, w3, dx, og, base, out):
         def per_group(name):
             return [sb.tile([P, N], F32, name="%s%d" % (name, g)) for g in groups]
 
-        halves = [slice(h * HALF, (h + 1) * HALF) for h in range(2)]
+        def both_groups(name):
+            return sb.tile([P, G, N], F32, name=name)
+
+        x_raw = sb.tile([P, PACK, N], F32)
+        nc.sync.dma_start(out=x_raw[:], in_=by_partition(x))
         w_raw = [sb.tile([P, PACK, M], F32, name="w_raw%d" % b) for b in range(3)]
-        x_raw = [sb.tile([P, PACK, HALF], F32, name="x_raw%d" % h) for h in range(2)]
+        for b, w in enumerate((w1, w2, w3)):
+            nc.sync.dma_start(out=w_raw[b][:], in_=by_partition(w))
         dx_raw = [sb.tile([P, PACK, HALF], F32, name="dx_raw%d" % h) for h in range(2)]
-        nc.sync.dma_start(out=w_raw[0][:], in_=by_partition(w1))
         for h in range(2):
-            nc.sync.dma_start(out=x_raw[h][:], in_=by_partition(x)[:, :, halves[h]])
-        nc.sync.dma_start(out=w_raw[1][:], in_=by_partition(w2))
-        nc.sync.dma_start(out=w_raw[2][:], in_=by_partition(w3))
-        for h in range(2):
-            nc.sync.dma_start(out=dx_raw[h][:], in_=by_partition(dx)[:, :, halves[h]])
+            nc.sync.dma_start(out=dx_raw[h][:], in_=by_partition(dx)[:, :, h * HALF : (h + 1) * HALF])
         base_sb = sb.tile([P, G, N], F32)
         nc.sync.dma_start(out=base_sb[:], in_=base.rearrange("g m n -> m g n"))
         gain = sb.tile([P, G], F32)
         with nc.allow_non_contiguous_dma(reason="one gain per output feature, one per partition"):
             nc.sync.dma_start(out=gain[:], in_=og.rearrange("g m o -> m (g o)"))
 
-        x_bf = [sb.tile([P, HALF, PACK], BF16, align_bytes=64, name="x_bf%d" % h) for h in range(2)]
         x_codes = sb.tile([P, N], U32, align_bytes=64)
         x_scales = sb.tile([P, N], U8, align_bytes=64)
-        dx_bf = [sb.tile([P, HALF, PACK], BF16, align_bytes=64, name="dx_bf%d" % h) for h in range(2)]
+        dx_cols = [slice(0, 256), slice(256, 384), slice(384, 512)]
+        x_bf = [
+            sb.tile([P, c.stop - c.start, PACK], BF16, align_bytes=64, name="x_bf%d" % c.start) for c in dx_cols
+        ]
+        dx_bf = [
+            sb.tile([P, c.stop - c.start, PACK], BF16, align_bytes=64, name="dx_bf%d" % c.start) for c in dx_cols
+        ]
         dx_codes = sb.tile([P, N], U32, align_bytes=64)
         dx_scales = sb.tile([P, N], U8, align_bytes=64)
         w_bf = [sb.tile([P, M, PACK], BF16, align_bytes=64, name="w_bf%d" % b) for b in range(3)]
@@ -93,67 +102,66 @@ def tile_rows_tnsoftmaxthree_kernel(tc, x, w1, w2, w3, dx, og, base, out):
                 stop=True,
             )
 
-        interleave(nc.scalar.copy, w_bf[0][:], w_raw[0][:])
-        quantize(nc, w_codes[0][:], w_scales[0][:], w_bf[0])
-        interleave(nc.vector.tensor_copy, x_bf[0][:, :X_VECTOR_COLS, :], x_raw[0][:, :, :X_VECTOR_COLS])
-        interleave(nc.scalar.copy, x_bf[0][:, X_VECTOR_COLS:, :], x_raw[0][:, :, X_VECTOR_COLS:])
-        quantize(nc, x_codes[:, halves[0]], x_scales[:, halves[0]], x_bf[0])
-        interleave(nc.vector.tensor_copy, x_bf[1][:, :X_VECTOR_COLS, :], x_raw[1][:, :, :X_VECTOR_COLS])
-        interleave(nc.scalar.copy, x_bf[1][:, X_VECTOR_COLS:, :], x_raw[1][:, :, X_VECTOR_COLS:])
-        quantize(nc, x_codes[:, halves[1]], x_scales[:, halves[1]], x_bf[1])
+        interleave(nc.scalar.copy, x_bf[0][:], x_raw[:, :, dx_cols[0]])
         interleave(nc.scalar.copy, w_bf[1][:], w_raw[1][:])
+        for piece in (1, 2):
+            interleave(nc.vector.tensor_copy, x_bf[piece][:], x_raw[:, :, dx_cols[piece]])
+        interleave(nc.vector.tensor_copy, w_bf[0][:], w_raw[0][:])
+        for piece in (1, 2):
+            quantize(nc, x_codes[:, dx_cols[piece]], x_scales[:, dx_cols[piece]], x_bf[piece])
+        quantize(nc, w_codes[0][:], w_scales[0][:], w_bf[0])
+        quantize(nc, x_codes[:, dx_cols[0]], x_scales[:, dx_cols[0]], x_bf[0])
         interleave(nc.vector.tensor_copy, w_bf[2][:], w_raw[2][:])
         quantize(nc, w_codes[1][:], w_scales[1][:], w_bf[1])
         quantize(nc, w_codes[2][:], w_scales[2][:], w_bf[2])
 
-        e = [per_group("e1_"), per_group("e2_"), per_group("e3_")]
+        e = [both_groups("e1"), both_groups("e2"), both_groups("e3")]
         for b in range(3):
             for g in groups:
                 product(z[g][b], g, b, x_codes, x_scales)
-                nc.scalar.activation(out=e[b][g][:], in_=z[g][b][:], func=ACT.Exp)
+                nc.scalar.activation(out=e[b][:, g, :], in_=z[g][b][:], func=ACT.Exp)
+                if (b, g) == (1, 0):
+                    interleave(nc.scalar.copy, dx_bf[2][:], dx_raw[1][:, :, M:])
         th, th2 = per_group("th"), per_group("th2")
         for g in groups:
             nc.scalar.activation(out=th[g][:], in_=z[g][0][:], func=ACT.Tanh)
         for g in groups:
             nc.scalar.activation(out=th2[g][:], in_=th[g][:], func=ACT.Square)
 
-        for h in range(2):
-            interleave(nc.vector.tensor_copy, dx_bf[h][:], dx_raw[h][:])
-            quantize(nc, dx_codes[:, halves[h]], dx_scales[:, halves[h]], dx_bf[h])
-        for g in groups:
-            for b in range(2):
+        interleave(nc.vector.tensor_copy, dx_bf[0][:], dx_raw[0][:])
+        quantize(nc, dx_codes[:, dx_cols[0]], dx_scales[:, dx_cols[0]], dx_bf[0])
+        interleave(nc.vector.tensor_copy, dx_bf[1][:], dx_raw[1][:, :, :M])
+        for piece in (1, 2):
+            quantize(nc, dx_codes[:, dx_cols[piece]], dx_scales[:, dx_cols[piece]], dx_bf[piece])
+        for b in range(3):
+            for g in groups:
                 product(tz[g][b], g, b, dx_codes, dx_scales)
-        for g in groups:
-            product(tz[g][2], g, 2, dx_codes, dx_scales)
 
-        e12, se = per_group("e12_"), per_group("se")
+        e12, se = both_groups("e12"), both_groups("se")
         for g in groups:
-            nc.vector.tensor_tensor(out=e12[g][:], in0=e[0][g][:], in1=e[1][g][:], op=ALU.add)
-        for g in groups:
-            nc.gpsimd.tensor_tensor(out=se[g][:], in0=e12[g][:], in1=e[2][g][:], op=ALU.add)
+            nc.vector.tensor_tensor(out=e12[:, g, :], in0=e[0][:, g, :], in1=e[1][:, g, :], op=ALU.add)
+        nc.gpsimd.tensor_tensor(out=se[:], in0=e12[:], in1=e[2][:], op=ALU.add)
 
         lse, inv = per_group("lse"), per_group("inv")
         for g in groups:
-            nc.scalar.activation(out=lse[g][:], in_=se[g][:], func=ACT.Ln)
+            nc.scalar.activation(out=lse[g][:], in_=se[:, g, :], func=ACT.Ln)
         for g in groups:
             nc.scalar.activation(out=inv[g][:], in_=lse[g][:], func=ACT.Exp, scale=-1.0)
 
-        a = [per_group("a1_"), per_group("a2_"), per_group("a3_")]
-        for g in groups:
-            for b in range(2):
-                nc.vector.tensor_tensor(out=a[b][g][:], in0=tz[g][b][:], in1=e[b][g][:], op=ALU.mult)
-        for g in groups:
-            nc.vector.tensor_tensor(out=a[2][g][:], in0=tz[g][2][:], in1=e[2][g][:], op=ALU.mult)
+        a = [both_groups("a1"), both_groups("a2"), both_groups("a3")]
+        for b in range(3):
+            for g in groups:
+                nc.vector.tensor_tensor(out=a[b][:, g, :], in0=tz[g][b][:], in1=e[b][:, g, :], op=ALU.mult)
         dth = per_group("dth")
         for g in groups:
             nc.vector.scalar_tensor_tensor(
                 out=dth[g][:], in0=th2[g][:], scalar=-1.0, in1=tz[g][0][:], op0=ALU.add, op1=ALU.mult
             )
-        a12, xse = per_group("a12_"), per_group("xse")
+        a12, xse = both_groups("a12"), per_group("xse")
+        for engine, cols in ((nc.gpsimd, slice(0, POOL_COLS)), (nc.vector, slice(POOL_COLS, G * N))):
+            engine.tensor_tensor(out=flat(a12)[:, cols], in0=flat(a[0])[:, cols], in1=flat(a[1])[:, cols], op=ALU.add)
         for g in groups:
-            nc.gpsimd.tensor_tensor(out=a12[g][:], in0=a[0][g][:], in1=a[1][g][:], op=ALU.add)
-        for g in groups:
-            nc.vector.tensor_tensor(out=xse[g][:], in0=a12[g][:], in1=a[2][g][:], op=ALU.add)
+            nc.vector.tensor_tensor(out=xse[g][:], in0=a12[:, g, :], in1=a[2][:, g, :], op=ALU.add)
         second, rest, first, ratio, y = (per_group(s) for s in ("second", "rest", "first", "ratio", "y"))
         for g in groups:
             nc.vector.scalar_tensor_tensor(

@@ -103,7 +103,8 @@ def tile_rows_tnsoftmaxthree_kernel(tc, x, w1, w2, w3, dx, og, base, out):
             )
 
         interleave(nc.scalar.copy, x_bf[0][:], x_raw[:, :, dx_cols[0]])
-        interleave(nc.scalar.copy, w_bf[1][:], w_raw[1][:])
+        for b in (1, 2):
+            interleave(nc.scalar.copy, w_bf[b][:], w_raw[b][:])
         for piece in (1, 2):
             interleave(nc.vector.tensor_copy, x_bf[piece][:], x_raw[:, :, dx_cols[piece]])
         interleave(nc.vector.tensor_copy, w_bf[0][:], w_raw[0][:])
@@ -111,7 +112,6 @@ def tile_rows_tnsoftmaxthree_kernel(tc, x, w1, w2, w3, dx, og, base, out):
             quantize(nc, x_codes[:, dx_cols[piece]], x_scales[:, dx_cols[piece]], x_bf[piece])
         quantize(nc, w_codes[0][:], w_scales[0][:], w_bf[0])
         quantize(nc, x_codes[:, dx_cols[0]], x_scales[:, dx_cols[0]], x_bf[0])
-        interleave(nc.vector.tensor_copy, w_bf[2][:], w_raw[2][:])
         quantize(nc, w_codes[1][:], w_scales[1][:], w_bf[1])
         quantize(nc, w_codes[2][:], w_scales[2][:], w_bf[2])
 
@@ -120,8 +120,6 @@ def tile_rows_tnsoftmaxthree_kernel(tc, x, w1, w2, w3, dx, og, base, out):
             for g in groups:
                 product(z[g][b], g, b, x_codes, x_scales)
                 nc.scalar.activation(out=e[b][:, g, :], in_=z[g][b][:], func=ACT.Exp)
-                if (b, g) == (1, 0):
-                    interleave(nc.scalar.copy, dx_bf[2][:], dx_raw[1][:, :, M:])
         th, th2 = per_group("th"), per_group("th2")
         for g in groups:
             nc.scalar.activation(out=th[g][:], in_=z[g][0][:], func=ACT.Tanh)
@@ -131,6 +129,7 @@ def tile_rows_tnsoftmaxthree_kernel(tc, x, w1, w2, w3, dx, og, base, out):
         interleave(nc.vector.tensor_copy, dx_bf[0][:], dx_raw[0][:])
         quantize(nc, dx_codes[:, dx_cols[0]], dx_scales[:, dx_cols[0]], dx_bf[0])
         interleave(nc.vector.tensor_copy, dx_bf[1][:], dx_raw[1][:, :, :M])
+        interleave(nc.vector.tensor_copy, dx_bf[2][:], dx_raw[1][:, :, M:])
         for piece in (1, 2):
             quantize(nc, dx_codes[:, dx_cols[piece]], dx_scales[:, dx_cols[piece]], dx_bf[piece])
         for b in range(3):
@@ -142,52 +141,51 @@ def tile_rows_tnsoftmaxthree_kernel(tc, x, w1, w2, w3, dx, og, base, out):
             nc.vector.tensor_tensor(out=e12[:, g, :], in0=e[0][:, g, :], in1=e[1][:, g, :], op=ALU.add)
         nc.gpsimd.tensor_tensor(out=se[:], in0=e12[:], in1=e[2][:], op=ALU.add)
 
-        lse, inv = per_group("lse"), per_group("inv")
+        lse, inv = both_groups("lse"), per_group("inv")
+        nc.scalar.activation(out=lse[:], in_=se[:], func=ACT.Ln)
         for g in groups:
-            nc.scalar.activation(out=lse[g][:], in_=se[:, g, :], func=ACT.Ln)
-        for g in groups:
-            nc.scalar.activation(out=inv[g][:], in_=lse[g][:], func=ACT.Exp, scale=-1.0)
+            nc.scalar.activation(out=inv[g][:], in_=lse[:, g, :], func=ACT.Exp, scale=-1.0)
 
         a = [both_groups("a1"), both_groups("a2"), both_groups("a3")]
         for b in range(3):
             for g in groups:
                 nc.vector.tensor_tensor(out=a[b][:, g, :], in0=tz[g][b][:], in1=e[b][:, g, :], op=ALU.mult)
-        dth = per_group("dth")
+        dth = both_groups("dth")
         for g in groups:
             nc.vector.scalar_tensor_tensor(
-                out=dth[g][:], in0=th2[g][:], scalar=-1.0, in1=tz[g][0][:], op0=ALU.add, op1=ALU.mult
+                out=dth[:, g, :], in0=th2[g][:], scalar=-1.0, in1=tz[g][0][:], op0=ALU.add, op1=ALU.mult
             )
-        a12, xse = both_groups("a12"), per_group("xse")
+        a12, xse = both_groups("a12"), both_groups("xse")
         for engine, cols in ((nc.gpsimd, slice(0, POOL_COLS)), (nc.vector, slice(POOL_COLS, G * N))):
             engine.tensor_tensor(out=flat(a12)[:, cols], in0=flat(a[0])[:, cols], in1=flat(a[1])[:, cols], op=ALU.add)
         for g in groups:
-            nc.vector.tensor_tensor(out=xse[g][:], in0=a12[:, g, :], in1=a[2][:, g, :], op=ALU.add)
-        second, rest, first, ratio, y = (per_group(s) for s in ("second", "rest", "first", "ratio", "y"))
-        for g in groups:
-            nc.vector.scalar_tensor_tensor(
-                out=second[g][:], in0=dth[g][:], scalar=gain[:, g : g + 1], in1=lse[g][:],
-                op0=ALU.mult, op1=ALU.mult,
-            )
-        for g in groups:
-            nc.vector.scalar_tensor_tensor(
-                out=first[g][:], in0=xse[g][:], scalar=gain[:, g : g + 1], in1=th[g][:],
-                op0=ALU.mult, op1=ALU.mult,
-            )
+            nc.vector.tensor_tensor(out=xse[:, g, :], in0=a12[:, g, :], in1=a[2][:, g, :], op=ALU.add)
+        second = both_groups("second")
+        rest, first, ratio, y = (per_group(s) for s in ("rest", "first", "ratio", "y"))
 
-        def add_base(g):
-            nc.vector.tensor_tensor(out=rest[g][:], in0=base_sb[:, g, :], in1=second[g][:], op=ALU.subtract)
+        def take_base(g):
+            nc.vector.scalar_tensor_tensor(
+                out=rest[g][:], in0=second[:, g, :], scalar=gain[:, g : g + 1], in1=base_sb[:, g, :],
+                op0=ALU.mult, op1=ALU.subtract,
+            )
 
         def divide(g, cols):
             nc.vector.tensor_tensor(out=ratio[g][:, cols], in0=first[g][:, cols], in1=inv[g][:, cols], op=ALU.mult)
 
         def finish(g, cols, queue):
-            nc.vector.tensor_tensor(out=y[g][:, cols], in0=ratio[g][:, cols], in1=rest[g][:, cols], op=ALU.add)
+            nc.vector.scalar_tensor_tensor(
+                out=y[g][:, cols], in0=ratio[g][:, cols], scalar=gain[:, g : g + 1], in1=rest[g][:, cols],
+                op0=ALU.mult, op1=ALU.subtract,
+            )
             queue.dma_start(out=out[g, :, cols], in_=y[g][:, cols])
 
         whole, head, tail = slice(0, N), slice(0, N - M), slice(N - M, N)
-        add_base(0)
+        nc.vector.tensor_tensor(out=first[0][:], in0=xse[:, 0, :], in1=th[0][:], op=ALU.mult)
+        nc.vector.tensor_tensor(out=second[:], in0=dth[:], in1=lse[:], op=ALU.mult)
+        nc.vector.tensor_tensor(out=first[1][:], in0=xse[:, 1, :], in1=th[1][:], op=ALU.mult)
+        take_base(0)
         divide(0, whole)
-        add_base(1)
+        take_base(1)
         finish(0, whole, nc.sync)
         divide(1, head)
         divide(1, tail)

from contextlib import ExitStack

import concourse.mybir as mybir

G, D, M, N = 2, 256, 128, 512
FLOPS = 6 * 2 * G * D * M * N

F32 = mybir.dt.float32
BF16 = mybir.dt.bfloat16
U32 = mybir.dt.uint32
U8 = mybir.dt.uint8
FP8X4 = mybir.dt.float8_e4m3fn_x4
ACT = mybir.ActivationFunctionType
ALU = mybir.AluOpType

P = 128
PACK = 4
ROWS = D // PACK
RUN = 4
HALF = N // 2
POOL_COLS = 768


def by_partition(src):
    return src.rearrange("g (p j) c -> (g p) j c", j=PACK)


def interleave(copy, packed, raw):
    copy(
        out=packed.rearrange("p (c i) j -> p c j i", i=RUN),
        in_=raw.rearrange("p j (c i) -> p c j i", i=RUN),
    )


def flat(tile):
    return tile[:].rearrange("p g n -> p (g n)")


def quantize(nc, codes, scales, packed):
    nc.vector.quantize_mx(
        out=codes.bitcast(FP8X4), scales=scales, in_=packed[:].rearrange("p c j -> p (c j)")
    )


def tile_rows_tnsoftmaxthree_kernel(tc, x, w1, w2, w3, dx, og, base, out):
    nc = tc.nc
    groups = range(G)

    with ExitStack() as ctx:
        sb = ctx.enter_context(tc.tile_pool(name="sb", bufs=1))
        ps = ctx.enter_context(tc.psum_pool(name="ps", bufs=1))
        ctx.enter_context(tc.manual_schedule())

        def per_group(name):
            return [sb.tile([P, N], F32, name="%s%d" % (name, g)) for g in groups]

        def both_groups(name):
            return sb.tile([P, G, N], F32, name=name)

        x_raw = sb.tile([P, PACK, N], F32)
        nc.sync.dma_start(out=x_raw[:], in_=by_partition(x))
        w_raw = [sb.tile([P, PACK, M], F32, name="w_raw%d" % b) for b in range(3)]
        for b, w in enumerate((w1, w2, w3)):
            nc.sync.dma_start(out=w_raw[b][:], in_=by_partition(w))
        dx_raw = [sb.tile([P, PACK, HALF], F32, name="dx_raw%d" % h) for h in range(2)]
        for h in range(2):
            nc.sync.dma_start(out=dx_raw[h][:], in_=by_partition(dx)[:, :, h * HALF : (h + 1) * HALF])
        base_sb = sb.tile([P, G, N], F32)
        nc.sync.dma_start(out=base_sb[:], in_=base.rearrange("g m n -> m g n"))
        gain = sb.tile([P, G], F32)
        with nc.allow_non_contiguous_dma(reason="one gain per output feature, one per partition"):
            nc.sync.dma_start(out=gain[:], in_=og.rearrange("g m o -> m (g o)"))

        x_codes = sb.tile([P, N], U32, align_bytes=64)
        x_scales = sb.tile([P, N], U8, align_bytes=64)
        dx_cols = [slice(0, 256), slice(256, 384), slice(384, 512)]
        x_bf = [
            sb.tile([P, c.stop - c.start, PACK], BF16, align_bytes=64, name="x_bf%d" % c.start) for c in dx_cols
        ]
        dx_bf = [
            sb.tile([P, c.stop - c.start, PACK], BF16, align_bytes=64, name="dx_bf%d" % c.start) for c in dx_cols
        ]
        dx_codes = sb.tile([P, N], U32, align_bytes=64)
        dx_scales = sb.tile([P, N], U8, align_bytes=64)
        w_bf = [sb.tile([P, M, PACK], BF16, align_bytes=64, name="w_bf%d" % b) for b in range(3)]
        w_codes = [sb.tile([P, M], U32, align_bytes=64, name="w_codes%d" % b) for b in range(3)]
        w_scales = [sb.tile([P, M], U8, align_bytes=64, name="w_scales%d" % b) for b in range(3)]

        bank = [[ps.tile([P, N], F32, name="bank%d_%d" % (g, i)) for i in range(4)] for g in groups]
        z = [[bank[g][0], bank[g][1], bank[g][2]] for g in groups]
        tz = [[bank[g][3], bank[g][1], bank[g][2]] for g in groups]

        def product(acc, g, b, codes, scales):
            rows = slice(g * ROWS, (g + 1) * ROWS)
            nc.tensor.matmul_mx(
                out=acc[:],
                lhsT=w_codes[b][rows, :].bitcast(FP8X4),
                lhsT_scale=w_scales[b][rows, :],
                rhs=codes[rows, :].bitcast(FP8X4),
                rhs_scale=scales[rows, :],
                start=True,
                stop=True,
            )

        interleave(nc.scalar.copy, x_bf[0][:], x_raw[:, :, dx_cols[0]])
        for b in (1, 2):
            interleave(nc.scalar.copy, w_bf[b][:], w_raw[b][:])
        for piece in (1, 2):
            interleave(nc.vector.tensor_copy, x_bf[piece][:], x_raw[:, :, dx_cols[piece]])
        interleave(nc.vector.tensor_copy, w_bf[0][:], w_raw[0][:])
        for piece in (1, 2):
            quantize(nc, x_codes[:, dx_cols[piece]], x_scales[:, dx_cols[piece]], x_bf[piece])
        quantize(nc, w_codes[0][:], w_scales[0][:], w_bf[0])
        quantize(nc, x_codes[:, dx_cols[0]], x_scales[:, dx_cols[0]], x_bf[0])
        quantize(nc, w_codes[1][:], w_scales[1][:], w_bf[1])
        quantize(nc, w_codes[2][:], w_scales[2][:], w_bf[2])

        e = [both_groups("e1"), both_groups("e2"), both_groups("e3")]
        for b in range(3):
            for g in groups:
                product(z[g][b], g, b, x_codes, x_scales)
                nc.scalar.activation(out=e[b][:, g, :], in_=z[g][b][:], func=ACT.Exp)
        th, th2 = per_group("th"), per_group("th2")
        for g in groups:
            nc.scalar.activation(out=th[g][:], in_=z[g][0][:], func=ACT.Tanh)
        for g in groups:
            nc.scalar.activation(out=th2[g][:], in_=th[g][:], func=ACT.Square)

        interleave(nc.vector.tensor_copy, dx_bf[0][:], dx_raw[0][:])
        quantize(nc, dx_codes[:, dx_cols[0]], dx_scales[:, dx_cols[0]], dx_bf[0])
        interleave(nc.vector.tensor_copy, dx_bf[1][:], dx_raw[1][:, :, :M])
        interleave(nc.vector.tensor_copy, dx_bf[2][:], dx_raw[1][:, :, M:])
        for piece in (1, 2):
            quantize(nc, dx_codes[:, dx_cols[piece]], dx_scales[:, dx_cols[piece]], dx_bf[piece])
        for b in range(3):
            for g in groups:
                product(tz[g][b], g, b, dx_codes, dx_scales)

        e12, se = both_groups("e12"), both_groups("se")
        for g in groups:
            nc.vector.tensor_tensor(out=e12[:, g, :], in0=e[0][:, g, :], in1=e[1][:, g, :], op=ALU.add)
        nc.gpsimd.tensor_tensor(out=se[:], in0=e12[:], in1=e[2][:], op=ALU.add)

        lse, inv = both_groups("lse"), per_group("inv")
        nc.scalar.activation(out=lse[:], in_=se[:], func=ACT.Ln)
        for g in groups:
            nc.scalar.activation(out=inv[g][:], in_=lse[:, g, :], func=ACT.Exp, scale=-1.0)

        a = [both_groups("a1"), both_groups("a2"), both_groups("a3")]
        for b in range(3):
            for g in groups:
                nc.vector.tensor_tensor(out=a[b][:, g, :], in0=tz[g][b][:], in1=e[b][:, g, :], op=ALU.mult)
        dth = both_groups("dth")
        for g in groups:
            nc.vector.scalar_tensor_tensor(
                out=dth[:, g, :], in0=th2[g][:], scalar=-1.0, in1=tz[g][0][:], op0=ALU.add, op1=ALU.mult
            )
        a12, xse = both_groups("a12"), both_groups("xse")
        for engine, cols in ((nc.gpsimd, slice(0, POOL_COLS)), (nc.vector, slice(POOL_COLS, G * N))):
            engine.tensor_tensor(out=flat(a12)[:, cols], in0=flat(a[0])[:, cols], in1=flat(a[1])[:, cols], op=ALU.add)
        for g in groups:
            nc.vector.tensor_tensor(out=xse[:, g, :], in0=a12[:, g, :], in1=a[2][:, g, :], op=ALU.add)
        second = both_groups("second")
        rest, first, ratio, y = (per_group(s) for s in ("rest", "first", "ratio", "y"))

        def take_base(g):
            nc.vector.scalar_tensor_tensor(
                out=rest[g][:], in0=second[:, g, :], scalar=gain[:, g : g + 1], in1=base_sb[:, g, :],
                op0=ALU.mult, op1=ALU.subtract,
            )

        def divide(g, cols):
            nc.vector.tensor_tensor(out=ratio[g][:, cols], in0=first[g][:, cols], in1=inv[g][:, cols], op=ALU.mult)

        def finish(g, cols, queue):
            nc.vector.scalar_tensor_tensor(
                out=y[g][:, cols], in0=ratio[g][:, cols], scalar=gain[:, g : g + 1], in1=rest[g][:, cols],
                op0=ALU.mult, op1=ALU.subtract,
            )
            queue.dma_start(out=out[g, :, cols], in_=y[g][:, cols])

        whole, head, tail = slice(0, N), slice(0, N - M), slice(N - M, N)
        nc.vector.tensor_tensor(out=first[0][:], in0=xse[:, 0, :], in1=th[0][:], op=ALU.mult)
        nc.vector.tensor_tensor(out=second[:], in0=dth[:], in1=lse[:], op=ALU.mult)
        nc.vector.tensor_tensor(out=first[1][:], in0=xse[:, 1, :], in1=th[1][:], op=ALU.mult)
        take_base(0)
        divide(0, whole)
        take_base(1)
        finish(0, whole, nc.sync)
        divide(1, head)
        divide(1, tail)
        finish(1, head, nc.scalar)
        finish(1, tail, nc.sync)
